import numpy as np
import ml_dtypes

BF16 = ml_dtypes.bfloat16


def bf(x):
    return np.asarray(x, np.float32).astype(BF16)


def f32(x):
    return np.asarray(x, np.float32)


def f64(x):
    return np.asarray(x).astype(np.float64)


def striped(idx):
    return np.tile(idx.reshape(-1, 16).T, (8, 1))


def rows(idx, k):
    return np.tile(idx, (k, 1))


def look(tab, idx):
    return np.take_along_axis(f64(tab), rows(idx, len(tab)), axis=1)


K, S, V, N = 128, 2048, 1536, 1536


def setup_inputs():
    return {"tab": f32(np.random.standard_normal((2, K, S))), "y": f32(np.random.standard_normal((K, V))), "offs": striped(np.random.permutation(S)[:N])}


def reference(tab, y, offs):
    idx = offs[:16].T.reshape(-1)
    x = (look(tab[0], idx) * f64(y)) * (np.maximum(look(tab[1], idx), 0.0))
    return x

@@ -1,0 +1,40 @@
+import concourse.mybir as mybir
+
+F32, U16 = mybir.dt.float32, mybir.dt.uint16
+MULT = mybir.AluOpType.mult
+RELU = mybir.ActivationFunctionType.Relu
+
+PIECE = 512
+PER_COLUMN = 16
+
+
+def tile_lookup_vg_mulrelu_out_kernel(tc, tab, y, offs, out):
+    nc = tc.nc
+    rows, places = tab.shape[1], tab.shape[2]
+    entries = y.shape[1]
+
+    with tc.tile_pool(name="held", bufs=1) as held:
+        offsets = held.tile([rows, entries // PER_COLUMN], U16, name="offsets")
+        values = held.tile([rows, places], F32, name="values")
+        gates = held.tile([rows, places], F32, name="gates")
+        stream = held.tile([rows, entries], F32, name="stream")
+        weighted = held.tile([rows, entries], F32, name="weighted")
+        opened = held.tile([rows, entries], F32, name="opened")
+        result = held.tile([rows, entries], F32, name="result")
+
+        nc.sync.dma_start(offsets[:], offs)
+        nc.sync.dma_start(values[:], tab[0])
+        nc.sync.dma_start(stream[:], y)
+        nc.sync.dma_start(gates[:], tab[1])
+
+        for start in range(0, entries, PIECE):
+            piece = slice(start, start + PIECE)
+            lists = offsets[:, start // PER_COLUMN : (start + PIECE) // PER_COLUMN]
+            nc.vector.tensor_tensor(weighted[:, piece], values[:].indirect(lists), stream[:, piece], MULT)
+
+        for start in range(0, entries, PIECE):
+            piece = slice(start, start + PIECE)
+            lists = offsets[:, start // PER_COLUMN : (start + PIECE) // PER_COLUMN]
+            nc.scalar.activation(opened[:, piece], gates[:].indirect(lists), RELU)
+            nc.vector.tensor_tensor(result[:, piece], weighted[:, piece], opened[:, piece], MULT)
+            nc.sync.dma_start(out[:, piece], result[:, piece])

@@ -22,6 +22,11 @@ def tile_lookup_vg_mulrelu_out_kernel(tc, tab, y, offs, out):
         opened = held.tile([rows, entries], F32, name="opened")
         result = held.tile([rows, entries], F32, name="result")
 
+        warm_in = held.tile([rows, 8], F32, name="warm_in")
+        warm_out = held.tile([rows, 8], F32, name="warm_out")
+        nc.gpsimd.memset(warm_in[:], 0.0)
+        nc.scalar.activation(warm_out[:], warm_in[:], RELU)
+
         nc.sync.dma_start(offsets[:], offs)
         nc.sync.dma_start(values[:], tab[0])
         nc.sync.dma_start(stream[:], y)

@@ -29,8 +29,10 @@ def tile_lookup_vg_mulrelu_out_kernel(tc, tab, y, offs, out):
 
         nc.sync.dma_start(offsets[:], offs)
         nc.sync.dma_start(values[:], tab[0])
-        nc.sync.dma_start(stream[:], y)
+        last = slice(entries - PIECE, entries)
+        nc.sync.dma_start(stream[:, : last.start], y[:, : last.start])
         nc.sync.dma_start(gates[:], tab[1])
+        nc.sync.dma_start(stream[:, last], y[:, last])
 
         for start in range(0, entries, PIECE):
             piece = slice(start, start + PIECE)

import concourse.mybir as mybir

F32, U16 = mybir.dt.float32, mybir.dt.uint16
MULT = mybir.AluOpType.mult
RELU = mybir.ActivationFunctionType.Relu

PIECE = 512
PER_COLUMN = 16


def tile_lookup_vg_mulrelu_out_kernel(tc, tab, y, offs, out):
    nc = tc.nc
    rows, places = tab.shape[1], tab.shape[2]
    entries = y.shape[1]

    with tc.tile_pool(name="held", bufs=1) as held:
        offsets = held.tile([rows, entries // PER_COLUMN], U16, name="offsets")
        values = held.tile([rows, places], F32, name="values")
        gates = held.tile([rows, places], F32, name="gates")
        stream = held.tile([rows, entries], F32, name="stream")
        weighted = held.tile([rows, entries], F32, name="weighted")
        opened = held.tile([rows, entries], F32, name="opened")
        result = held.tile([rows, entries], F32, name="result")

        warm_in = held.tile([rows, 8], F32, name="warm_in")
        warm_out = held.tile([rows, 8], F32, name="warm_out")
        nc.gpsimd.memset(warm_in[:], 0.0)
        nc.scalar.activation(warm_out[:], warm_in[:], RELU)

        nc.sync.dma_start(offsets[:], offs)
        nc.sync.dma_start(values[:], tab[0])
        last = slice(entries - PIECE, entries)
        nc.sync.dma_start(stream[:, : last.start], y[:, : last.start])
        nc.sync.dma_start(gates[:], tab[1])
        nc.sync.dma_start(stream[:, last], y[:, last])

        for start in range(0, entries, PIECE):
            piece = slice(start, start + PIECE)
            lists = offsets[:, start // PER_COLUMN : (start + PIECE) // PER_COLUMN]
            nc.vector.tensor_tensor(weighted[:, piece], values[:].indirect(lists), stream[:, piece], MULT)

        for start in range(0, entries, PIECE):
            piece = slice(start, start + PIECE)
            lists = offsets[:, start // PER_COLUMN : (start + PIECE) // PER_COLUMN]
            nc.scalar.activation(opened[:, piece], gates[:].indirect(lists), RELU)
            nc.vector.tensor_tensor(result[:, piece], weighted[:, piece], opened[:, piece], MULT)
            nc.sync.dma_start(out[:, piece], result[:, piece])
